import numpy as np
import ml_dtypes

BF16 = ml_dtypes.bfloat16


def bf(x):
    return np.asarray(x, np.float32).astype(BF16)


def f32(x):
    return np.asarray(x, np.float32)


def f64(x):
    return np.asarray(x).astype(np.float64)


def striped(idx):
    return np.tile(idx.reshape(-1, 16).T, (8, 1))


S, K, M, N, E, Q, O = 512, 256, 128, 256, 4, 64, 256


def sigmoid(v):
    return 1.0 / (1.0 + np.exp(-v))


def setup_inputs():
    return {"base": bf(np.random.standard_normal((M, S))), "x": bf(np.random.standard_normal((K, N))), "w": bf(1.2 * np.random.standard_normal((E, K, M)) / np.sqrt(K)), "w2": bf(np.random.standard_normal((M, O)) / np.sqrt(2 * M)), "b": f32(0.5 * np.random.standard_normal((O, 1))), "offs": striped(np.random.permutation(S)[:N])}


def reference(base, x, w, w2, b, offs):
    idx = offs[:16].T.reshape(-1)
    z = f64(base).copy()
    for e in range(E):
        z[:, idx[e * Q : (e + 1) * Q]] += f64(w)[e].T @ f64(x)[:, e * Q : (e + 1) * Q]
    y = f64(w2).T @ z
    return (y + f64(b)) * sigmoid(y + f64(b))

@@ -1,0 +1,64 @@
+import concourse.mybir as mybir
+from concourse.masks import make_identity
+
+BF16, F32, U16 = mybir.dt.bfloat16, mybir.dt.float32, mybir.dt.uint16
+SILU = mybir.ActivationFunctionType.Silu
+
+P = 128
+S = 512
+K = 256
+N = 256
+E = 4
+Q = N // E
+O = 256
+KB = K // P
+OB = O // P
+LANES = 16
+
+FLOPS = 2 * P * K * N + 2 * P * O * S
+
+
+def tile_rows_thenproj_silu_kernel(tc, base, x, w, w2, b, offs, out):
+    nc = tc.nc
+    with (
+        tc.tile_pool(name="held", bufs=1) as held,
+        tc.psum_pool(name="psum", bufs=1) as psum,
+    ):
+        base_tile = held.tile([P, S], BF16)
+        x_tile = held.tile([P, KB * N], BF16)
+        offsets = held.tile([P, N // LANES], U16)
+        w_tile = held.tile([P, E, KB * P], BF16)
+        w2_tile = held.tile([P, O], BF16)
+        bias = held.tile([P, OB], F32)
+        nc.sync.dma_start(base_tile[:], base)
+        nc.sync.dma_start(x_tile[:], x.rearrange("(p c) n -> p (c n)", c=KB))
+        nc.sync.dma_start(offsets[:], offs)
+        nc.sync.dma_start(w_tile[:], w.rearrange("e (p c) m -> p e (c m)", c=KB))
+        nc.scalar.dma_start(w2_tile[:], w2)
+        nc.scalar.dma_start(bias[:], b.rearrange("(a p) o -> p (a o)", p=P))
+
+        identity = held.tile([P, P], BF16)
+        make_identity(nc, identity[:])
+
+        window = psum.tile([P, S], F32)
+        nc.tensor.matmul(window[:], identity[:], base_tile[:], start=True, stop=False)
+
+        for e in range(E):
+            piece = offsets[:, e * Q // LANES : (e + 1) * Q // LANES]
+            for c in range(KB):
+                nc.tensor.matmul(
+                    window[:].indirect(piece),
+                    w_tile[:, e, c * P : (c + 1) * P],
+                    x_tile[:, c * N + e * Q : c * N + (e + 1) * Q],
+                    start=False,
+                    stop=(e == E - 1 and c == KB - 1),
+                )
+
+        z = held.tile([P, S], BF16)
+        nc.vector.tensor_copy(z[:], window[:])
+        for a in range(OB):
+            y = psum.tile([P, S], F32, name=f"y{a}")
+            nc.tensor.matmul(y[:], w2_tile[:, a * P : (a + 1) * P], z[:], start=True, stop=True)
+            result = held.tile([P, S], F32, name=f"result{a}")
+            nc.scalar.activation(result[:], y[:], SILU, bias=bias[:, a : a + 1])
+            nc.sync.dma_start(out[a * P : (a + 1) * P, :], result[:])

@@ -13,6 +13,7 @@ Q = N // E
 O = 256
 KB = K // P
 OB = O // P
+WARM_UPS = 4
 LANES = 16
 
 FLOPS = 2 * P * K * N + 2 * P * O * S
@@ -24,6 +25,14 @@ def tile_rows_thenproj_silu_kernel(tc, base, x, w, w2, b, offs, out):
         tc.tile_pool(name="held", bufs=1) as held,
         tc.psum_pool(name="psum", bufs=1) as psum,
     ):
+        zeros = held.tile([P, S], BF16)
+        nc.vector.memset(zeros[:], 0.0)
+        silu_of_zero = held.tile([P, 1], F32)
+        nc.scalar.activation(silu_of_zero[:], zeros[:, 0:1], SILU)
+        spare = psum.tile([P, S], F32)
+        for turn in range(WARM_UPS):
+            nc.tensor.matmul(spare[:], zeros[:, 0:P], zeros[:], start=True, stop=True)
+
         base_tile = held.tile([P, S], BF16)
         x_tile = held.tile([P, KB * N], BF16)
         offsets = held.tile([P, N // LANES], U16)

@@ -14,6 +14,7 @@ O = 256
 KB = K // P
 OB = O // P
 WARM_UPS = 4
+HALVES = 2
 LANES = 16
 
 FLOPS = 2 * P * K * N + 2 * P * O * S
@@ -43,8 +44,8 @@ def tile_rows_thenproj_silu_kernel(tc, base, x, w, w2, b, offs, out):
         nc.sync.dma_start(x_tile[:], x.rearrange("(p c) n -> p (c n)", c=KB))
         nc.sync.dma_start(offsets[:], offs)
         nc.sync.dma_start(w_tile[:], w.rearrange("e (p c) m -> p e (c m)", c=KB))
-        nc.scalar.dma_start(w2_tile[:], w2)
-        nc.scalar.dma_start(bias[:], b.rearrange("(a p) o -> p (a o)", p=P))
+        nc.sync.dma_start(w2_tile[:], w2)
+        nc.sync.dma_start(bias[:], b.rearrange("(a p) o -> p (a o)", p=P))
 
         identity = held.tile([P, P], BF16)
         make_identity(nc, identity[:])
@@ -63,11 +64,14 @@ def tile_rows_thenproj_silu_kernel(tc, base, x, w, w2, b, offs, out):
                     stop=(e == E - 1 and c == KB - 1),
                 )
 
-        z = held.tile([P, S], BF16)
-        nc.vector.tensor_copy(z[:], window[:])
+        results = [held.tile([P, S], F32, name=f"result{a}") for a in range(OB)]
+        for h in range(HALVES):
+            columns = slice(h * S // HALVES, (h + 1) * S // HALVES)
+            z = held.tile([P, S // HALVES], BF16, name=f"z{h}")
+            nc.vector.tensor_copy(z[:], window[:, columns])
+            for a in range(OB):
+                y = psum.tile([P, S // HALVES], F32, name=f"y{h}{a}")
+                nc.tensor.matmul(y[:], w2_tile[:, a * P : (a + 1) * P], z[:], start=True, stop=True)
+                nc.scalar.activation(results[a][:, columns], y[:], SILU, bias=bias[:, a : a + 1])
         for a in range(OB):
-            y = psum.tile([P, S], F32, name=f"y{a}")
-            nc.tensor.matmul(y[:], w2_tile[:, a * P : (a + 1) * P], z[:], start=True, stop=True)
-            result = held.tile([P, S], F32, name=f"result{a}")
-            nc.scalar.activation(result[:], y[:], SILU, bias=bias[:, a : a + 1])
-            nc.sync.dma_start(out[a * P : (a + 1) * P, :], result[:])
+            nc.sync.dma_start(out[a * P : (a + 1) * P, :], results[a][:])

@@ -13,7 +13,8 @@ Q = N // E
 O = 256
 KB = K // P
 OB = O // P
-WARM_UPS = 4
+WARM_COLUMNS = 256
+WARM_UPS = 6
 HALVES = 2
 LANES = 16
 
@@ -26,11 +27,11 @@ def tile_rows_thenproj_silu_kernel(tc, base, x, w, w2, b, offs, out):
         tc.tile_pool(name="held", bufs=1) as held,
         tc.psum_pool(name="psum", bufs=1) as psum,
     ):
-        zeros = held.tile([P, S], BF16)
+        zeros = held.tile([P, WARM_COLUMNS], BF16)
         nc.vector.memset(zeros[:], 0.0)
         silu_of_zero = held.tile([P, 1], F32)
         nc.scalar.activation(silu_of_zero[:], zeros[:, 0:1], SILU)
-        spare = psum.tile([P, S], F32)
+        spare = psum.tile([P, WARM_COLUMNS], F32)
         for turn in range(WARM_UPS):
             nc.tensor.matmul(spare[:], zeros[:, 0:P], zeros[:], start=True, stop=True)
 
@@ -43,7 +44,10 @@ def tile_rows_thenproj_silu_kernel(tc, base, x, w, w2, b, offs, out):
         nc.sync.dma_start(base_tile[:], base)
         nc.sync.dma_start(x_tile[:], x.rearrange("(p c) n -> p (c n)", c=KB))
         nc.sync.dma_start(offsets[:], offs)
-        nc.sync.dma_start(w_tile[:], w.rearrange("e (p c) m -> p e (c m)", c=KB))
+        w_rows = w.rearrange("e (p c) m -> p e (c m)", c=KB)
+        for h in range(HALVES):
+            experts = slice(h * E // HALVES, (h + 1) * E // HALVES)
+            nc.sync.dma_start(w_tile[:, experts], w_rows[:, experts])
         nc.sync.dma_start(w2_tile[:], w2)
         nc.sync.dma_start(bias[:], b.rearrange("(a p) o -> p (a o)", p=P))
 
@@ -64,7 +68,6 @@ def tile_rows_thenproj_silu_kernel(tc, base, x, w, w2, b, offs, out):
                     stop=(e == E - 1 and c == KB - 1),
                 )
 
-        results = [held.tile([P, S], F32, name=f"result{a}") for a in range(OB)]
         for h in range(HALVES):
             columns = slice(h * S // HALVES, (h + 1) * S // HALVES)
             z = held.tile([P, S // HALVES], BF16, name=f"z{h}")
@@ -72,6 +75,6 @@ def tile_rows_thenproj_silu_kernel(tc, base, x, w, w2, b, offs, out):
             for a in range(OB):
                 y = psum.tile([P, S // HALVES], F32, name=f"y{h}{a}")
                 nc.tensor.matmul(y[:], w2_tile[:, a * P : (a + 1) * P], z[:], start=True, stop=True)
-                nc.scalar.activation(results[a][:, columns], y[:], SILU, bias=bias[:, a : a + 1])
-        for a in range(OB):
-            nc.sync.dma_start(out[a * P : (a + 1) * P, :], results[a][:])
+                result = held.tile([P, S // HALVES], F32, name=f"result{h}{a}")
+                nc.scalar.activation(result[:], y[:], SILU, bias=bias[:, a : a + 1])
+                nc.sync.dma_start(out[a * P : (a + 1) * P, columns], result[:])

import concourse.mybir as mybir
from concourse.masks import make_identity

BF16, F32, U16 = mybir.dt.bfloat16, mybir.dt.float32, mybir.dt.uint16
SILU = mybir.ActivationFunctionType.Silu

P = 128
S = 512
K = 256
N = 256
E = 4
Q = N // E
O = 256
KB = K // P
OB = O // P
WARM_COLUMNS = 256
WARM_UPS = 6
HALVES = 2
LANES = 16

FLOPS = 2 * P * K * N + 2 * P * O * S


def tile_rows_thenproj_silu_kernel(tc, base, x, w, w2, b, offs, out):
    nc = tc.nc
    with (
        tc.tile_pool(name="held", bufs=1) as held,
        tc.psum_pool(name="psum", bufs=1) as psum,
    ):
        zeros = held.tile([P, WARM_COLUMNS], BF16)
        nc.vector.memset(zeros[:], 0.0)
        silu_of_zero = held.tile([P, 1], F32)
        nc.scalar.activation(silu_of_zero[:], zeros[:, 0:1], SILU)
        spare = psum.tile([P, WARM_COLUMNS], F32)
        for turn in range(WARM_UPS):
            nc.tensor.matmul(spare[:], zeros[:, 0:P], zeros[:], start=True, stop=True)

        base_tile = held.tile([P, S], BF16)
        x_tile = held.tile([P, KB * N], BF16)
        offsets = held.tile([P, N // LANES], U16)
        w_tile = held.tile([P, E, KB * P], BF16)
        w2_tile = held.tile([P, O], BF16)
        bias = held.tile([P, OB], F32)
        nc.sync.dma_start(base_tile[:], base)
        nc.sync.dma_start(x_tile[:], x.rearrange("(p c) n -> p (c n)", c=KB))
        nc.sync.dma_start(offsets[:], offs)
        w_rows = w.rearrange("e (p c) m -> p e (c m)", c=KB)
        for h in range(HALVES):
            experts = slice(h * E // HALVES, (h + 1) * E // HALVES)
            nc.sync.dma_start(w_tile[:, experts], w_rows[:, experts])
        nc.sync.dma_start(w2_tile[:], w2)
        nc.sync.dma_start(bias[:], b.rearrange("(a p) o -> p (a o)", p=P))

        identity = held.tile([P, P], BF16)
        make_identity(nc, identity[:])

        window = psum.tile([P, S], F32)
        nc.tensor.matmul(window[:], identity[:], base_tile[:], start=True, stop=False)

        for e in range(E):
            piece = offsets[:, e * Q // LANES : (e + 1) * Q // LANES]
            for c in range(KB):
                nc.tensor.matmul(
                    window[:].indirect(piece),
                    w_tile[:, e, c * P : (c + 1) * P],
                    x_tile[:, c * N + e * Q : c * N + (e + 1) * Q],
                    start=False,
                    stop=(e == E - 1 and c == KB - 1),
                )

        for h in range(HALVES):
            columns = slice(h * S // HALVES, (h + 1) * S // HALVES)
            z = held.tile([P, S // HALVES], BF16, name=f"z{h}")
            nc.vector.tensor_copy(z[:], window[:, columns])
            for a in range(OB):
                y = psum.tile([P, S // HALVES], F32, name=f"y{h}{a}")
                nc.tensor.matmul(y[:], w2_tile[:, a * P : (a + 1) * P], z[:], start=True, stop=True)
                result = held.tile([P, S // HALVES], F32, name=f"result{h}{a}")
                nc.scalar.activation(result[:], y[:], SILU, bias=bias[:, a : a + 1])
                nc.sync.dma_start(out[a * P : (a + 1) * P, columns], result[:])
